import numpy as np
import ml_dtypes


def mxq(x, axis, fmt="e4m3"):
    dtype, down = {"e4m3": (ml_dtypes.float8_e4m3fn, 7), "e5m2": (ml_dtypes.float8_e5m2, 14)}[fmt]
    v = np.moveaxis(np.asarray(x, np.float32).astype(ml_dtypes.bfloat16).astype(np.float64), axis, -1)
    blocks = v.reshape(v.shape[:-1] + (-1, 32))
    amax = np.abs(blocks).max(-1, keepdims=True)
    byte = np.maximum(np.where(amax > 0, np.frexp(amax)[1] - 1 + 127, 0) - down, 1)
    scale = np.exp2(byte - 127.0)
    codes = (blocks / scale).astype(np.float32).astype(dtype).astype(np.float64)
    return np.moveaxis((codes * scale).reshape(v.shape), -1, axis)


WIDE = False


def mx_kscale(k, group=512):
    if not WIDE:
        return np.ones(k)
    levels = np.array([10, -10, 5, -5, 0])
    if group != 512:
        return np.exp2(np.random.permutation(np.resize(levels, k // group))).repeat(group)
    if k % 512:
        return np.exp2(np.random.permutation(np.resize(levels, k // 32))).repeat(32)
    a = np.empty((k // 512, 16))
    for p in range(k // 512):
        a[p, :8] = np.random.permutation(np.resize(levels, 8))
        for g in range(8):
            far = levels[np.abs(levels - a[p, g]) >= 10]
            a[p, g + 8] = far[np.random.randint(len(far))]
    return np.exp2(a.ravel()).repeat(32)


def f64(x):
    return np.asarray(x).astype(np.float64)


G, D, M, N = 2, 256, 128, 512


def setup_inputs():
    n = np.random.standard_normal
    s_d = mx_kscale(D, 0)
    return {
        "x": (n((G, D, M)) / s_d[:, None] / np.sqrt(D)).astype(np.float32),
        "c": (n((G, D, N)) * s_d[:, None]).astype(np.float32),
    }


def reference(x, c):
    xq = mxq(f64(x), 1, "e4m3")
    cq = mxq(f64(c), 1, "e4m3")
    z = xq.transpose(0, 2, 1) @ cq
    p = np.square(np.maximum(z, 0.0))
    s = np.sum(p, axis=-1, keepdims=True)
    y = p / (s + 0.01)
    return y

@@ -1,0 +1,131 @@
+from contextlib import ExitStack
+
+import concourse.mybir as mybir
+
+G, D, M, N = 2, 256, 128, 512
+FLOPS = 2 * G * D * M * N
+
+F32 = mybir.dt.float32
+BF16 = mybir.dt.bfloat16
+U32 = mybir.dt.uint32
+U8 = mybir.dt.uint8
+FP8X4 = mybir.dt.float8_e4m3fn_x4
+ACT = mybir.ActivationFunctionType
+ALU = mybir.AluOpType
+AX = mybir.AxisListType
+
+P = 128
+PACK = 4
+ROWS = D // PACK
+W = 128
+CHUNKS = N // W
+EPS = 0.01
+RUN = 4
+
+
+def interleave(eng_copy, grouped, raw):
+    eng_copy(
+        out=grouped.rearrange("p (c i) t -> p c t i", i=RUN),
+        in_=raw.rearrange("p t (c i) -> p c t i", i=RUN),
+    )
+
+
+def tile_rows_relusum_kernel(tc, x, c, out):
+    nc = tc.nc
+    xv = x.rearrange("g (p t) m -> (g p) t m", t=PACK)
+    cv = c.rearrange("g (p t) n -> (g p) t n", t=PACK)
+    with ExitStack() as ctx:
+        sb = ctx.enter_context(tc.tile_pool(name="sb", bufs=1))
+        ps = ctx.enter_context(tc.psum_pool(name="ps", bufs=1))
+        ctx.enter_context(tc.manual_schedule())
+
+        x_raw = sb.tile([P, PACK, M], F32, name="x_raw")
+        nc.sync.dma_start(out=x_raw[:], in_=xv)
+        c_raw = []
+        for k in range(CHUNKS):
+            t = sb.tile([P, PACK, W], F32, name="c_raw%d" % k)
+            nc.sync.dma_start(out=t[:], in_=cv[:, :, k * W : (k + 1) * W])
+            c_raw.append(t)
+
+        ones = sb.tile([P, G, 1], F32, name="ones")
+        nc.vector.memset(ones[:], 1.0)
+        part = sb.tile([P, G, CHUNKS + 1], F32, name="part")
+        nc.scalar.activation(out=part[:, :, CHUNKS : CHUNKS + 1], in_=ones[:], func=ACT.Copy, scale=EPS)
+
+        def operand(name, width):
+            grouped = sb.tile([P, width, PACK], BF16, name=name + "_bf", align_bytes=64)
+            codes = sb.tile([P, width], U32, name=name + "_codes", align_bytes=64)
+            scales = sb.tile([P, width], U8, name=name + "_scales", align_bytes=64)
+            return grouped, codes, scales
+
+        def quantize(op):
+            grouped, codes, scales = op
+            nc.vector.quantize_mx(out=codes[:].bitcast(FP8X4), scales=scales[:], in_=grouped[:].rearrange("p w t -> p (w t)"))
+
+        xo = operand("x", M)
+        co = [operand("c%d" % k, W) for k in range(CHUNKS)]
+        z = [[ps.tile([M, 512], F32, name="z%d_%d" % (g, k)) for k in range(CHUNKS)] for g in range(G)]
+        r = [sb.tile([M, N], F32, name="r%d" % g) for g in range(G)]
+        sq = [sb.tile([M, N], F32, name="sq%d" % g) for g in range(G)]
+        y = [sb.tile([M, N], F32, name="y%d" % g) for g in range(G)]
+
+        def mm(k):
+            for g in range(G):
+                rows = slice(g * ROWS, (g + 1) * ROWS)
+                nc.tensor.matmul_mx(
+                    out=z[g][k][:, 0:W],
+                    lhsT=xo[1][rows, :].bitcast(FP8X4),
+                    lhsT_scale=xo[2][rows, :],
+                    rhs=co[k][1][rows, :].bitcast(FP8X4),
+                    rhs_scale=co[k][2][rows, :],
+                    start=True,
+                    stop=True,
+                )
+
+        def cols(k):
+            return slice(k * W, (k + 1) * W)
+
+        def relu_s(g, k):
+            nc.scalar.activation(out=r[g][:, cols(k)], in_=z[g][k][:, 0:W], func=ACT.Relu)
+
+        def relu_v(g, k):
+            nc.vector.tensor_scalar(out=r[g][:, cols(k)], in0=z[g][k][:, 0:W], scalar1=0.0, scalar2=None, op0=ALU.max)
+
+        def square_s(g, k):
+            nc.scalar.activation(out=sq[g][:, cols(k)], in_=r[g][:, cols(k)], func=ACT.Square, accum_out=part[:, g, k : k + 1])
+
+        def square_v(g, k):
+            nc.vector.scalar_tensor_tensor(
+                out=sq[g][:, cols(k)], in0=r[g][:, cols(k)], scalar=1.0, in1=r[g][:, cols(k)],
+                op0=ALU.mult, op1=ALU.mult, accum_out=part[:, g, k : k + 1],
+            )
+
+        last = CHUNKS - 1
+        interleave(nc.vector.tensor_copy, xo[0][:], x_raw[:])
+        quantize(xo)
+        for k in range(CHUNKS):
+            interleave(nc.vector.tensor_copy, co[k][0][:], c_raw[k][:])
+            quantize(co[k])
+            mm(k)
+            if k >= 1:
+                square_v(0, k - 1)
+            if k < last:
+                relu_s(0, k)
+                relu_s(1, k)
+                square_s(1, k)
+        relu_v(0, last)
+        relu_s(1, last)
+        square_v(0, last)
+        square_s(1, last)
+
+        total = sb.tile([P, G], F32, name="total")
+        nc.vector.tensor_reduce(out=total[:], in_=part[:], axis=AX.X, op=ALU.add)
+        inv = sb.tile([P, G], F32, name="inv")
+        nc.vector.reciprocal(out=inv[:], in_=total[:])
+
+        H = N // 2
+        nc.vector.tensor_scalar(out=y[0][:], in0=sq[0][:], scalar1=inv[:, 0:1], scalar2=None, op0=ALU.mult)
+        nc.scalar.activation(out=y[1][:, 0:H], in_=sq[1][:, 0:H], func=ACT.Copy, scale=inv[:, 1:2])
+        nc.sync.dma_start(out=out[0], in_=y[0][:])
+        nc.vector.tensor_scalar(out=y[1][:, H:N], in0=sq[1][:, H:N], scalar1=inv[:, 1:2], scalar2=None, op0=ALU.mult)
+        nc.scalar.dma_start(out=out[1], in_=y[1][:])

@@ -18,9 +18,9 @@ P = 128
 PACK = 4
 ROWS = D // PACK
 W = 128
-CHUNKS = N // W
 EPS = 0.01
 RUN = 4
+PAD = 8
 
 
 def interleave(eng_copy, grouped, raw):
@@ -39,93 +39,110 @@ def tile_rows_relusum_kernel(tc, x, c, out):
         ps = ctx.enter_context(tc.psum_pool(name="ps", bufs=1))
         ctx.enter_context(tc.manual_schedule())
 
-        x_raw = sb.tile([P, PACK, M], F32, name="x_raw")
-        nc.sync.dma_start(out=x_raw[:], in_=xv)
-        c_raw = []
-        for k in range(CHUNKS):
-            t = sb.tile([P, PACK, W], F32, name="c_raw%d" % k)
-            nc.sync.dma_start(out=t[:], in_=cv[:, :, k * W : (k + 1) * W])
-            c_raw.append(t)
+        def load(name, src, lo, hi, eng):
+            t = sb.tile([P, PACK, hi - lo], F32, name=name)
+            eng.dma_start(out=t[:], in_=src[:, :, lo:hi])
+            return t
 
-        ones = sb.tile([P, G, 1], F32, name="ones")
-        nc.vector.memset(ones[:], 1.0)
-        part = sb.tile([P, G, CHUNKS + 1], F32, name="part")
-        nc.scalar.activation(out=part[:, :, CHUNKS : CHUNKS + 1], in_=ones[:], func=ACT.Copy, scale=EPS)
+        ca = load("ca", cv, 0, 256, nc.sync)
+        x_raw = load("x_raw", xv, 0, M, nc.sync)
+        cb = load("cb", cv, 256, 384, nc.sync)
+        cd = load("cd", cv, 384, 512, nc.sync)
 
-        def operand(name, width):
-            grouped = sb.tile([P, width, PACK], BF16, name=name + "_bf", align_bytes=64)
-            codes = sb.tile([P, width], U32, name=name + "_codes", align_bytes=64)
-            scales = sb.tile([P, width], U8, name=name + "_scales", align_bytes=64)
-            return grouped, codes, scales
-
-        def quantize(op):
-            grouped, codes, scales = op
-            nc.vector.quantize_mx(out=codes[:].bitcast(FP8X4), scales=scales[:], in_=grouped[:].rearrange("p w t -> p (w t)"))
-
-        xo = operand("x", M)
-        co = [operand("c%d" % k, W) for k in range(CHUNKS)]
-        z = [[ps.tile([M, 512], F32, name="z%d_%d" % (g, k)) for k in range(CHUNKS)] for g in range(G)]
-        r = [sb.tile([M, N], F32, name="r%d" % g) for g in range(G)]
-        sq = [sb.tile([M, N], F32, name="sq%d" % g) for g in range(G)]
+        r = [sb.tile([M, PAD + N], F32, name="r%d" % g) for g in range(G)]
+        sq = [sb.tile([M, PAD + N], F32, name="sq%d" % g) for g in range(G)]
         y = [sb.tile([M, N], F32, name="y%d" % g) for g in range(G)]
+        ones = sb.tile([P, 1], F32, name="ones")
+        nc.vector.memset(ones[:], 1.0)
+        for g in range(G):
+            nc.scalar.activation(out=r[g][:, PAD - 1 : PAD], in_=ones[:], func=ACT.Abs_reciprocal_sqrt, scale=1.0 / EPS)
+        early = sb.tile([P, G], F32, name="early")
+        late = sb.tile([P, G], F32, name="late")
+        inv = sb.tile([P, G], F32, name="inv")
 
-        def mm(k):
+        xg = sb.tile([P, M, PACK], BF16, name="xg", align_bytes=64)
+        xc = sb.tile([P, M], U32, name="xc", align_bytes=64)
+        xs = sb.tile([P, M], U8, name="xs", align_bytes=64)
+        cg = sb.tile([P, N, PACK], BF16, name="cg", align_bytes=64)
+        cc = sb.tile([P, N], U32, name="cc", align_bytes=64)
+        cs = sb.tile([P, N], U8, name="cs", align_bytes=64)
+
+        def quantize(grouped, codes, scales, lo, hi):
+            nc.vector.quantize_mx(out=codes[:, lo:hi].bitcast(FP8X4), scales=scales[:, lo:hi], in_=grouped[:, lo:hi, :].rearrange("p w t -> p (w t)"))
+
+        z = [[ps.tile([M, 512], F32, name="z%d_%d" % (g, b)) for b in range(4)] for g in range(G)]
+
+        def mm(lo, bank, at):
             for g in range(G):
                 rows = slice(g * ROWS, (g + 1) * ROWS)
                 nc.tensor.matmul_mx(
-                    out=z[g][k][:, 0:W],
-                    lhsT=xo[1][rows, :].bitcast(FP8X4),
-                    lhsT_scale=xo[2][rows, :],
-                    rhs=co[k][1][rows, :].bitcast(FP8X4),
-                    rhs_scale=co[k][2][rows, :],
+                    out=z[g][bank][:, at : at + W],
+                    lhsT=xc[rows, :].bitcast(FP8X4),
+                    lhsT_scale=xs[rows, :],
+                    rhs=cc[rows, lo : lo + W].bitcast(FP8X4),
+                    rhs_scale=cs[rows, lo : lo + W],
                     start=True,
                     stop=True,
                 )
 
-        def cols(k):
-            return slice(k * W, (k + 1) * W)
+        def relu_s(g, bank, lo, hi):
+            nc.scalar.activation(out=r[g][:, PAD + lo : PAD + hi], in_=z[g][bank][:, 0 : hi - lo], func=ACT.Relu)
 
-        def relu_s(g, k):
-            nc.scalar.activation(out=r[g][:, cols(k)], in_=z[g][k][:, 0:W], func=ACT.Relu)
+        def relu_v(g, bank, lo, hi):
+            nc.vector.tensor_scalar(out=r[g][:, PAD + lo : PAD + hi], in0=z[g][bank][:, 0 : hi - lo], scalar1=0.0, scalar2=None, op0=ALU.max)
 
-        def relu_v(g, k):
-            nc.vector.tensor_scalar(out=r[g][:, cols(k)], in0=z[g][k][:, 0:W], scalar1=0.0, scalar2=None, op0=ALU.max)
+        def square_s(g, lo, hi, acc):
+            nc.scalar.activation(out=sq[g][:, PAD + lo : PAD + hi], in_=r[g][:, PAD + lo : PAD + hi], func=ACT.Square, accum_out=acc)
 
-        def square_s(g, k):
-            nc.scalar.activation(out=sq[g][:, cols(k)], in_=r[g][:, cols(k)], func=ACT.Square, accum_out=part[:, g, k : k + 1])
-
-        def square_v(g, k):
+        def square_v(g, lo, hi, acc):
             nc.vector.scalar_tensor_tensor(
-                out=sq[g][:, cols(k)], in0=r[g][:, cols(k)], scalar=1.0, in1=r[g][:, cols(k)],
-                op0=ALU.mult, op1=ALU.mult, accum_out=part[:, g, k : k + 1],
+                out=sq[g][:, PAD + lo : PAD + hi], in0=r[g][:, PAD + lo : PAD + hi], scalar=1.0, in1=r[g][:, PAD + lo : PAD + hi],
+                op0=ALU.mult, op1=ALU.mult, accum_out=acc,
             )
 
-        last = CHUNKS - 1
-        interleave(nc.vector.tensor_copy, xo[0][:], x_raw[:])
-        quantize(xo)
-        for k in range(CHUNKS):
-            interleave(nc.vector.tensor_copy, co[k][0][:], c_raw[k][:])
-            quantize(co[k])
-            mm(k)
-            if k >= 1:
-                square_v(0, k - 1)
-            if k < last:
-                relu_s(0, k)
-                relu_s(1, k)
-                square_s(1, k)
-        relu_v(0, last)
-        relu_s(1, last)
-        square_v(0, last)
-        square_s(1, last)
+        def ars(g):
+            nc.scalar.activation(out=inv[:, g : g + 1], in_=late[:, g : g + 1], func=ACT.Abs_reciprocal_sqrt, bias=early[:, g : g + 1])
 
-        total = sb.tile([P, G], F32, name="total")
-        nc.vector.tensor_reduce(out=total[:], in_=part[:], axis=AX.X, op=ALU.add)
-        inv = sb.tile([P, G], F32, name="inv")
-        nc.vector.reciprocal(out=inv[:], in_=total[:])
+        def scale_v(g, lo, hi):
+            nc.vector.tensor_scalar(out=y[g][:, lo:hi], in0=sq[g][:, PAD + lo : PAD + hi], scalar1=inv[:, g : g + 1], scalar2=inv[:, g : g + 1], op0=ALU.mult, op1=ALU.mult)
 
-        H = N // 2
-        nc.vector.tensor_scalar(out=y[0][:], in0=sq[0][:], scalar1=inv[:, 0:1], scalar2=None, op0=ALU.mult)
-        nc.scalar.activation(out=y[1][:, 0:H], in_=sq[1][:, 0:H], func=ACT.Copy, scale=inv[:, 1:2])
-        nc.sync.dma_start(out=out[0], in_=y[0][:])
-        nc.vector.tensor_scalar(out=y[1][:, H:N], in0=sq[1][:, H:N], scalar1=inv[:, 1:2], scalar2=None, op0=ALU.mult)
-        nc.scalar.dma_start(out=out[1], in_=y[1][:])
+        def scale_s(g, lo, hi):
+            nc.scalar.activation(out=y[g][:, lo:hi], in_=r[g][:, PAD + lo : PAD + hi], func=ACT.Square, scale=inv[:, g : g + 1])
+
+        def store(eng, g, lo, hi):
+            eng.dma_start(out=out[g, :, lo:hi], in_=y[g][:, lo:hi])
+
+        interleave(nc.vector.tensor_copy, cg[:, 0:176, :], ca[:, :, 0:176])
+        interleave(nc.scalar.copy, cg[:, 176:256, :], ca[:, :, 176:256])
+        interleave(nc.vector.tensor_copy, xg[:, 0:72, :], x_raw[:, :, 0:72])
+        interleave(nc.scalar.copy, xg[:, 72:128, :], x_raw[:, :, 72:128])
+        quantize(cg, cc, cs, 0, 256)
+        quantize(xg, xc, xs, 0, M)
+        mm(0, 0, 0)
+        mm(128, 0, 128)
+        relu_s(0, 0, 0, 256)
+        relu_s(1, 0, 0, 256)
+        interleave(nc.vector.tensor_copy, cg[:, 256:384, :], cb[:])
+        quantize(cg, cc, cs, 256, 384)
+        mm(256, 1, 0)
+        relu_s(0, 1, 256, 384)
+        relu_s(1, 1, 256, 384)
+        square_s(1, -1, 384, early[:, 1:2])
+        interleave(nc.vector.tensor_copy, cg[:, 384:512, :], cd[:])
+        quantize(cg, cc, cs, 384, 512)
+        mm(384, 2, 0)
+        square_v(0, -1, 384, early[:, 0:1])
+        relu_v(0, 2, 384, 512)
+        relu_s(1, 2, 384, 512)
+        square_v(0, 384, 512, late[:, 0:1])
+        square_s(1, 384, 512, late[:, 1:2])
+        ars(1)
+        ars(0)
+        scale_v(1, 256, 512)
+        scale_s(1, 0, 256)
+        store(nc.sync, 1, 256, 512)
+        scale_v(0, 0, 256)
+        store(nc.sync, 0, 0, 256)
+        store(nc.scalar, 1, 0, 256)
+        scale_v(0, 256, 512)
+        store(nc.sync, 0, 256, 512)

@@ -44,9 +44,8 @@ def tile_rows_relusum_kernel(tc, x, c, out):
             eng.dma_start(out=t[:], in_=src[:, :, lo:hi])
             return t
 
-        ca = load("ca", cv, 0, 256, nc.sync)
+        ca = load("ca", cv, 0, 384, nc.sync)
         x_raw = load("x_raw", xv, 0, M, nc.sync)
-        cb = load("cb", cv, 256, 384, nc.sync)
         cd = load("cd", cv, 384, 512, nc.sync)
 
         r = [sb.tile([M, PAD + N], F32, name="r%d" % g) for g in range(G)]
@@ -72,8 +71,8 @@ def tile_rows_relusum_kernel(tc, x, c, out):
 
         z = [[ps.tile([M, 512], F32, name="z%d_%d" % (g, b)) for b in range(4)] for g in range(G)]
 
-        def mm(lo, bank, at):
-            for g in range(G):
+        def mm1(g, lo, bank, at):
+            if True:
                 rows = slice(g * ROWS, (g + 1) * ROWS)
                 nc.tensor.matmul_mx(
                     out=z[g][bank][:, at : at + W],
@@ -85,11 +84,11 @@ def tile_rows_relusum_kernel(tc, x, c, out):
                     stop=True,
                 )
 
-        def relu_s(g, bank, lo, hi):
-            nc.scalar.activation(out=r[g][:, PAD + lo : PAD + hi], in_=z[g][bank][:, 0 : hi - lo], func=ACT.Relu)
+        def relu_s(g, bank, lo, hi, at=0):
+            nc.scalar.activation(out=r[g][:, PAD + lo : PAD + hi], in_=z[g][bank][:, at : at + hi - lo], func=ACT.Relu)
 
-        def relu_v(g, bank, lo, hi):
-            nc.vector.tensor_scalar(out=r[g][:, PAD + lo : PAD + hi], in0=z[g][bank][:, 0 : hi - lo], scalar1=0.0, scalar2=None, op0=ALU.max)
+        def relu_v(g, bank, lo, hi, at=0):
+            nc.vector.tensor_scalar(out=r[g][:, PAD + lo : PAD + hi], in0=z[g][bank][:, at : at + hi - lo], scalar1=0.0, scalar2=None, op0=ALU.max)
 
         def square_s(g, lo, hi, acc):
             nc.scalar.activation(out=sq[g][:, PAD + lo : PAD + hi], in_=r[g][:, PAD + lo : PAD + hi], func=ACT.Square, accum_out=acc)
@@ -112,37 +111,39 @@ def tile_rows_relusum_kernel(tc, x, c, out):
         def store(eng, g, lo, hi):
             eng.dma_start(out=out[g, :, lo:hi], in_=y[g][:, lo:hi])
 
-        interleave(nc.vector.tensor_copy, cg[:, 0:176, :], ca[:, :, 0:176])
-        interleave(nc.scalar.copy, cg[:, 176:256, :], ca[:, :, 176:256])
+        interleave(nc.vector.tensor_copy, cg[:, 0:264, :], ca[:, :, 0:264])
+        interleave(nc.scalar.copy, cg[:, 264:384, :], ca[:, :, 264:384])
         interleave(nc.vector.tensor_copy, xg[:, 0:72, :], x_raw[:, :, 0:72])
         interleave(nc.scalar.copy, xg[:, 72:128, :], x_raw[:, :, 72:128])
         quantize(cg, cc, cs, 0, 256)
-        quantize(xg, xc, xs, 0, M)
-        mm(0, 0, 0)
-        mm(128, 0, 128)
-        relu_s(0, 0, 0, 256)
-        relu_s(1, 0, 0, 256)
-        interleave(nc.vector.tensor_copy, cg[:, 256:384, :], cb[:])
+        quantize(xg, xc, xs, 0, 128)
+        interleave(nc.vector.tensor_copy, cg[:, 384:464, :], cd[:, :, 0:80])
+        interleave(nc.scalar.copy, cg[:, 464:512, :], cd[:, :, 80:128])
         quantize(cg, cc, cs, 256, 384)
-        mm(256, 1, 0)
-        relu_s(0, 1, 256, 384)
-        relu_s(1, 1, 256, 384)
-        square_s(1, -1, 384, early[:, 1:2])
-        interleave(nc.vector.tensor_copy, cg[:, 384:512, :], cd[:])
         quantize(cg, cc, cs, 384, 512)
-        mm(384, 2, 0)
-        square_v(0, -1, 384, early[:, 0:1])
-        relu_v(0, 2, 384, 512)
-        relu_s(1, 2, 384, 512)
-        square_v(0, 384, 512, late[:, 0:1])
-        square_s(1, 384, 512, late[:, 1:2])
-        ars(1)
+        mm1(0, 0, 0, 0)
+        mm1(0, 128, 0, 128)
+        mm1(0, 256, 1, 0)
+        mm1(1, 0, 0, 0)
+        mm1(0, 384, 2, 0)
+        mm1(1, 128, 0, 128)
+        mm1(1, 256, 1, 0)
+        mm1(1, 384, 1, 128)
+        relu_s(0, 0, 0, 256)
+        relu_s(0, 1, 256, 384)
+        relu_s(0, 2, 384, 512)
+        square_v(0, -1, 256, early[:, 0:1])
+        square_v(0, 256, 512, late[:, 0:1])
+        relu_s(1, 0, 0, 256)
+        relu_s(1, 1, 256, 512)
         ars(0)
-        scale_v(1, 256, 512)
-        scale_s(1, 0, 256)
-        store(nc.sync, 1, 256, 512)
+        square_v(1, -1, 256, early[:, 1:2])
+        square_s(1, 256, 512, late[:, 1:2])
         scale_v(0, 0, 256)
         store(nc.sync, 0, 0, 256)
-        store(nc.scalar, 1, 0, 256)
+        ars(1)
         scale_v(0, 256, 512)
         store(nc.sync, 0, 256, 512)
+        scale_s(1, 352, 512)
+        scale_v(1, 0, 352)
+        store(nc.sync, 1, 0, 512)

from contextlib import ExitStack

import concourse.mybir as mybir

G, D, M, N = 2, 256, 128, 512
FLOPS = 2 * G * D * M * N

F32 = mybir.dt.float32
BF16 = mybir.dt.bfloat16
U32 = mybir.dt.uint32
U8 = mybir.dt.uint8
FP8X4 = mybir.dt.float8_e4m3fn_x4
ACT = mybir.ActivationFunctionType
ALU = mybir.AluOpType
AX = mybir.AxisListType

P = 128
PACK = 4
ROWS = D // PACK
W = 128
EPS = 0.01
RUN = 4
PAD = 8


def interleave(eng_copy, grouped, raw):
    eng_copy(
        out=grouped.rearrange("p (c i) t -> p c t i", i=RUN),
        in_=raw.rearrange("p t (c i) -> p c t i", i=RUN),
    )


def tile_rows_relusum_kernel(tc, x, c, out):
    nc = tc.nc
    xv = x.rearrange("g (p t) m -> (g p) t m", t=PACK)
    cv = c.rearrange("g (p t) n -> (g p) t n", t=PACK)
    with ExitStack() as ctx:
        sb = ctx.enter_context(tc.tile_pool(name="sb", bufs=1))
        ps = ctx.enter_context(tc.psum_pool(name="ps", bufs=1))
        ctx.enter_context(tc.manual_schedule())

        def load(name, src, lo, hi, eng):
            t = sb.tile([P, PACK, hi - lo], F32, name=name)
            eng.dma_start(out=t[:], in_=src[:, :, lo:hi])
            return t

        ca = load("ca", cv, 0, 384, nc.sync)
        x_raw = load("x_raw", xv, 0, M, nc.sync)
        cd = load("cd", cv, 384, 512, nc.sync)

        r = [sb.tile([M, PAD + N], F32, name="r%d" % g) for g in range(G)]
        sq = [sb.tile([M, PAD + N], F32, name="sq%d" % g) for g in range(G)]
        y = [sb.tile([M, N], F32, name="y%d" % g) for g in range(G)]
        ones = sb.tile([P, 1], F32, name="ones")
        nc.vector.memset(ones[:], 1.0)
        for g in range(G):
            nc.scalar.activation(out=r[g][:, PAD - 1 : PAD], in_=ones[:], func=ACT.Abs_reciprocal_sqrt, scale=1.0 / EPS)
        early = sb.tile([P, G], F32, name="early")
        late = sb.tile([P, G], F32, name="late")
        inv = sb.tile([P, G], F32, name="inv")

        xg = sb.tile([P, M, PACK], BF16, name="xg", align_bytes=64)
        xc = sb.tile([P, M], U32, name="xc", align_bytes=64)
        xs = sb.tile([P, M], U8, name="xs", align_bytes=64)
        cg = sb.tile([P, N, PACK], BF16, name="cg", align_bytes=64)
        cc = sb.tile([P, N], U32, name="cc", align_bytes=64)
        cs = sb.tile([P, N], U8, name="cs", align_bytes=64)

        def quantize(grouped, codes, scales, lo, hi):
            nc.vector.quantize_mx(out=codes[:, lo:hi].bitcast(FP8X4), scales=scales[:, lo:hi], in_=grouped[:, lo:hi, :].rearrange("p w t -> p (w t)"))

        z = [[ps.tile([M, 512], F32, name="z%d_%d" % (g, b)) for b in range(4)] for g in range(G)]

        def mm1(g, lo, bank, at):
            if True:
                rows = slice(g * ROWS, (g + 1) * ROWS)
                nc.tensor.matmul_mx(
                    out=z[g][bank][:, at : at + W],
                    lhsT=xc[rows, :].bitcast(FP8X4),
                    lhsT_scale=xs[rows, :],
                    rhs=cc[rows, lo : lo + W].bitcast(FP8X4),
                    rhs_scale=cs[rows, lo : lo + W],
                    start=True,
                    stop=True,
                )

        def relu_s(g, bank, lo, hi, at=0):
            nc.scalar.activation(out=r[g][:, PAD + lo : PAD + hi], in_=z[g][bank][:, at : at + hi - lo], func=ACT.Relu)

        def relu_v(g, bank, lo, hi, at=0):
            nc.vector.tensor_scalar(out=r[g][:, PAD + lo : PAD + hi], in0=z[g][bank][:, at : at + hi - lo], scalar1=0.0, scalar2=None, op0=ALU.max)

        def square_s(g, lo, hi, acc):
            nc.scalar.activation(out=sq[g][:, PAD + lo : PAD + hi], in_=r[g][:, PAD + lo : PAD + hi], func=ACT.Square, accum_out=acc)

        def square_v(g, lo, hi, acc):
            nc.vector.scalar_tensor_tensor(
                out=sq[g][:, PAD + lo : PAD + hi], in0=r[g][:, PAD + lo : PAD + hi], scalar=1.0, in1=r[g][:, PAD + lo : PAD + hi],
                op0=ALU.mult, op1=ALU.mult, accum_out=acc,
            )

        def ars(g):
            nc.scalar.activation(out=inv[:, g : g + 1], in_=late[:, g : g + 1], func=ACT.Abs_reciprocal_sqrt, bias=early[:, g : g + 1])

        def scale_v(g, lo, hi):
            nc.vector.tensor_scalar(out=y[g][:, lo:hi], in0=sq[g][:, PAD + lo : PAD + hi], scalar1=inv[:, g : g + 1], scalar2=inv[:, g : g + 1], op0=ALU.mult, op1=ALU.mult)

        def scale_s(g, lo, hi):
            nc.scalar.activation(out=y[g][:, lo:hi], in_=r[g][:, PAD + lo : PAD + hi], func=ACT.Square, scale=inv[:, g : g + 1])

        def store(eng, g, lo, hi):
            eng.dma_start(out=out[g, :, lo:hi], in_=y[g][:, lo:hi])

        interleave(nc.vector.tensor_copy, cg[:, 0:264, :], ca[:, :, 0:264])
        interleave(nc.scalar.copy, cg[:, 264:384, :], ca[:, :, 264:384])
        interleave(nc.vector.tensor_copy, xg[:, 0:72, :], x_raw[:, :, 0:72])
        interleave(nc.scalar.copy, xg[:, 72:128, :], x_raw[:, :, 72:128])
        quantize(cg, cc, cs, 0, 256)
        quantize(xg, xc, xs, 0, 128)
        interleave(nc.vector.tensor_copy, cg[:, 384:464, :], cd[:, :, 0:80])
        interleave(nc.scalar.copy, cg[:, 464:512, :], cd[:, :, 80:128])
        quantize(cg, cc, cs, 256, 384)
        quantize(cg, cc, cs, 384, 512)
        mm1(0, 0, 0, 0)
        mm1(0, 128, 0, 128)
        mm1(0, 256, 1, 0)
        mm1(1, 0, 0, 0)
        mm1(0, 384, 2, 0)
        mm1(1, 128, 0, 128)
        mm1(1, 256, 1, 0)
        mm1(1, 384, 1, 128)
        relu_s(0, 0, 0, 256)
        relu_s(0, 1, 256, 384)
        relu_s(0, 2, 384, 512)
        square_v(0, -1, 256, early[:, 0:1])
        square_v(0, 256, 512, late[:, 0:1])
        relu_s(1, 0, 0, 256)
        relu_s(1, 1, 256, 512)
        ars(0)
        square_v(1, -1, 256, early[:, 1:2])
        square_s(1, 256, 512, late[:, 1:2])
        scale_v(0, 0, 256)
        store(nc.sync, 0, 0, 256)
        ars(1)
        scale_v(0, 256, 512)
        store(nc.sync, 0, 256, 512)
        scale_s(1, 352, 512)
        scale_v(1, 0, 352)
        store(nc.sync, 1, 0, 512)
